import numpy as np
import ml_dtypes


def mxq(x, axis, fmt="e4m3"):
    dtype, down = {"e4m3": (ml_dtypes.float8_e4m3fn, 7), "e5m2": (ml_dtypes.float8_e5m2, 14)}[fmt]
    v = np.moveaxis(np.asarray(x, np.float32).astype(ml_dtypes.bfloat16).astype(np.float64), axis, -1)
    blocks = v.reshape(v.shape[:-1] + (-1, 32))
    amax = np.abs(blocks).max(-1, keepdims=True)
    byte = np.maximum(np.where(amax > 0, np.frexp(amax)[1] - 1 + 127, 0) - down, 1)
    scale = np.exp2(byte - 127.0)
    codes = (blocks / scale).astype(np.float32).astype(dtype).astype(np.float64)
    return np.moveaxis((codes * scale).reshape(v.shape), -1, axis)


WIDE = False


def mx_kscale(k):
    if not WIDE:
        return np.ones(k)
    levels = np.array([10, -10, 5, -5, 0])
    if k % 512:
        return np.exp2(np.random.permutation(np.resize(levels, k // 32))).repeat(32)
    a = np.empty((k // 512, 16))
    for p in range(k // 512):
        a[p, :8] = np.random.permutation(np.resize(levels, 8))
        for g in range(8):
            far = levels[np.abs(levels - a[p, g]) >= 10]
            a[p, g + 8] = far[np.random.randint(len(far))]
    return np.exp2(a.ravel()).repeat(32)


def f64(x):
    return np.asarray(x).astype(np.float64)


def striped(idx):
    return np.tile(idx.reshape(-1, 16).T, (8, 1)).astype(np.uint16)


def unstriped(offs):
    return offs[:16].T.reshape(-1).astype(np.int64)


def d_silu(v):
    s = 1.0 / (1.0 + np.exp(-np.maximum(v, -700.0)))
    return s * (1.0 + v * (1.0 - s))


K, T, E, C, H, N = 128, 768, 6, 256, 512, 512


def by_expert(wq, xq):
    return np.concatenate([wq[e].T @ xq[:, e * C:(e + 1) * C] for e in range(E)], axis=1)


def setup_inputs():
    n = np.random.standard_normal
    s = mx_kscale(N)[:, None]
    u = mx_kscale(H)
    first = np.random.permutation(np.repeat(np.arange(E), T // E))
    second = (first + 1 + np.random.permutation(np.repeat(np.arange(E - 1), -(-T // (E - 1)))[:T])) % E
    while np.bincount(second, minlength=E).max() != T // E:
        load = np.bincount(second, minlength=E); hi, lo = int(load.argmax()), int(load.argmin())
        t = np.flatnonzero((second == hi) & (first != lo))[0]; second[t] = lo
    slot_token = np.empty(E * C, np.int64); pos = np.empty((2, T), np.int64); fill = np.zeros(E, np.int64)
    place = np.stack([np.random.permutation(C) for _ in range(E)])
    for r, deal in enumerate((first, second)):
        for t in np.random.permutation(T):
            e = deal[t]; j = e * C + place[e, fill[e]]; fill[e] += 1; slot_token[j] = t; pos[r, t] = j
    g = np.random.uniform(0.2, 0.8, T)
    w_slot = np.empty(E * C); w_slot[pos[0]] = g; w_slot[pos[1]] = 1.0 - g
    return {
        "dyT": (n((N, T)) * s).astype(np.float32),
        "a": n((H, E * C)).astype(np.float32),
        "w2": (n((E, N, H)) / np.sqrt(N) / s[None] * u[None, None, :]).astype(np.float32),
        "w1": (n((E, H, K)) / np.sqrt(H) / u[None, :, None]).astype(np.float32),
        "gate": np.tile(w_slot, (N, 1)).astype(np.float32),
        "offs": striped(slot_token),
        "pos1": striped(pos[0]),
        "pos2": striped(pos[1]),
    }


def reference(dyT, a, w2, w1, gate, offs, pos1, pos2):
    idx = unstriped(offs)
    gq = mxq(f64(gate) * f64(dyT)[:, idx], 0, "e4m3")
    dh = by_expert(mxq(f64(w2), 1, "e4m3"), gq)
    da = dh * d_silu(f64(a))
    dx = by_expert(mxq(f64(w1), 1, "e4m3"), mxq(da, 0, "e4m3"))
    return dx[:, unstriped(pos1)] + dx[:, unstriped(pos2)]

@@ -1,0 +1,261 @@
+from contextlib import ExitStack
+
+import concourse.mybir as mybir
+
+F32 = mybir.dt.float32
+BF16 = mybir.dt.bfloat16
+U32 = mybir.dt.uint32
+U16 = mybir.dt.uint16
+U8 = mybir.dt.uint8
+FP8X4 = mybir.dt.float8_e4m3fn_x4
+ADD = mybir.AluOpType.add
+SUB = mybir.AluOpType.subtract
+MULT = mybir.AluOpType.mult
+SIGMOID = mybir.ActivationFunctionType.Sigmoid
+SILU = mybir.ActivationFunctionType.Silu
+
+P = 128
+K, T, E, C, H, N = 128, 768, 6, 256, 512, 512
+SLOTS = E * C
+PAIRS = E // 2
+C2 = 2 * C
+HALF = 128
+
+FLOPS = 2 * SLOTS * H * (N + K)
+BYTES = 4 * (N * T + H * SLOTS + E * N * H + E * H * K + SLOTS + K * T) + 2 * P * (2 * SLOTS + 0) // 16
+
+W2_ON_VECTOR = (4,)
+
+
+def tile_moe_bdx_mlp_silu_kernel(tc, dyT, a, w2, w1, gate, offs, pos1, pos2, out):
+    nc = tc.nc
+    with ExitStack() as ctx:
+        lists = ctx.enter_context(tc.tile_pool(name="lists", bufs=1))
+        held = ctx.enter_context(tc.tile_pool(name="held", bufs=1))
+        ring2 = ctx.enter_context(tc.tile_pool(name="ring2", bufs=2))
+        ring3 = ctx.enter_context(tc.tile_pool(name="ring3", bufs=3))
+        psum_h = ctx.enter_context(tc.psum_pool(name="psum_h", bufs=5))
+        psum_x = ctx.enter_context(tc.psum_pool(name="psum_x", bufs=3))
+
+        offs_t = lists.tile([P, SLOTS // 16], U16, name="offs_t")
+        pos1_t = lists.tile([P, T // 16], U16, name="pos1_t")
+        pos2_t = lists.tile([P, T // 16], U16, name="pos2_t")
+        dy_t = [held.tile([P, T], F32, name=f"dy{t}") for t in range(4)]
+        gate_t = [held.tile([P, C2], F32, name=f"gate{q}") for q in range(PAIRS)]
+        a_t = [held.tile([P, 4, C2], F32, name=f"a{q}") for q in range(PAIRS)]
+        s_t = [held.tile([P, 4, C2], F32, name=f"s{q}") for q in range(PAIRS)]
+        w2_raw = [held.tile([P, 4, H], F32, name=f"w2_raw{e}") for e in range(E)]
+        w1_raw = [held.tile([P, 2, 4, K], F32, name=f"w1_raw{q}") for q in range(PAIRS)]
+        g_codes = [held.tile([P, C2], U32, align_bytes=64, name=f"g_codes{q}") for q in range(PAIRS)]
+        g_scales = [held.tile([P, C2], U8, align_bytes=64, name=f"g_scales{q}") for q in range(PAIRS)]
+        w2_codes = [held.tile([P, H], U32, align_bytes=64, name=f"w2_codes{e}") for e in range(E)]
+        w2_scales = [held.tile([P, H], U8, align_bytes=64, name=f"w2_scales{e}") for e in range(E)]
+        w1_codes = [held.tile([P, 2 * K], U32, align_bytes=64, name=f"w1_codes{q}") for q in range(PAIRS)]
+        w1_scales = [held.tile([P, 2 * K], U8, align_bytes=64, name=f"w1_scales{q}") for q in range(PAIRS)]
+        sig_t = [s_t[0], a_t[1], a_t[2]]
+        sil_t = [a_t[0], s_t[1], s_t[2]]
+        dx_all = held.tile([P, SLOTS], F32, name="dx_all")
+        warm = held.tile([P, 1], F32, name="warm")
+
+        nc.vector.memset(warm[:], 0.0)
+        nc.scalar.activation(warm[:], warm[:], SIGMOID)
+
+        dy_rows = dyT.rearrange("(p t) c -> t p c", t=4)
+        a_rows = a.rearrange("(p t) s -> p t s", t=4)
+
+        def load_dy(t):
+            nc.sync.dma_start(dy_t[t][:], dy_rows[t])
+
+        def load_gate(q):
+            nc.sync.dma_start(gate_t[q][:], gate[0:P, q * C2 : (q + 1) * C2])
+
+        def load_a(q, lo, hi):
+            nc.sync.dma_start(a_t[q][:, :, lo:hi], a_rows[:, :, q * C2 + lo : q * C2 + hi])
+
+        def load_w2(e):
+            nc.sync.dma_start(w2_raw[e][:], w2[e].rearrange("(p j) i -> p j i", j=4))
+
+        def load_w1(q):
+            nc.sync.dma_start(w1_raw[q][:], w1[2 * q : 2 * q + 2].rearrange("e (p j) k -> p e j k", j=4))
+
+        nc.sync.dma_start(offs_t[:], offs)
+        load_dy(0)
+        load_gate(0)
+        load_a(0, 0, C)
+        load_dy(1)
+        load_dy(2)
+        load_dy(3)
+        load_a(0, C, C2)
+        load_w2(0)
+        load_w1(0)
+        load_gate(1)
+        load_w2(1)
+        load_a(1, 0, C2)
+        load_a(2, 0, C2)
+        load_gate(2)
+        load_w2(2)
+        load_w1(1)
+        load_w2(3)
+        load_w2(4)
+        load_w1(2)
+        load_w2(5)
+        nc.sync.dma_start(pos1_t[:], pos1)
+        nc.sync.dma_start(pos2_t[:], pos2)
+
+        def gather(q):
+            g4 = ring2.tile([P, 4, C2], F32, name="g4")
+            for t in range(4):
+                nc.vector.tensor_tensor(
+                    g4[:, t, :],
+                    dy_t[t][:].indirect(offs_t[:, q * (C2 // 16) : (q + 1) * (C2 // 16)]),
+                    gate_t[q][:],
+                    MULT,
+                )
+            return g4
+
+        def cast_g(g4):
+            gb = ring2.tile([P, C2, 4], BF16, align_bytes=64, name="gb")
+            nc.scalar.copy(
+                gb[:].rearrange("p (c i) t -> p c t i", i=4), g4[:].rearrange("p t (c i) -> p c t i", i=4)
+            )
+            return gb
+
+        def quant_g(q, gb):
+            nc.vector.quantize_mx(
+                out=g_codes[q][:].bitcast(FP8X4), scales=g_scales[q][:], in_=gb[:].rearrange("p n j -> p (n j)")
+            )
+
+        def cast_w2(e):
+            w2b = ring3.tile([P, H, 4], BF16, align_bytes=64, name="w2b")
+            dst = w2b[:].rearrange("p (t m) j -> p m j t", t=4)
+            src = w2_raw[e][:].rearrange("p j (m t) -> p m j t", t=4)
+            if e in W2_ON_VECTOR:
+                nc.vector.tensor_copy(dst, src)
+            else:
+                nc.scalar.copy(dst, src)
+            return w2b
+
+        def quant_w2(e, w2b):
+            nc.vector.quantize_mx(
+                out=w2_codes[e][:].bitcast(FP8X4), scales=w2_scales[e][:], in_=w2b[:].rearrange("p i j -> p (i j)")
+            )
+
+        def cast_w1(q):
+            w1b = ring2.tile([P, 2, K, 4], BF16, align_bytes=64, name="w1b")
+            nc.vector.tensor_copy(
+                w1b[:].rearrange("p e (c i) j -> p e c j i", i=4),
+                w1_raw[q][:].rearrange("p e j (c i) -> p e c j i", i=4),
+            )
+            return w1b
+
+        def quant_w1(q, w1b):
+            nc.vector.quantize_mx(
+                out=w1_codes[q][:].bitcast(FP8X4), scales=w1_scales[q][:], in_=w1b[:].rearrange("p e k j -> p (e k j)")
+            )
+
+        def sigmoid(q, lo, hi):
+            nc.scalar.activation(sig_t[q][:, :, lo:hi], a_t[q][:, :, lo:hi], SIGMOID)
+
+        def silu_neg(q, lo, hi):
+            nc.scalar.activation(sil_t[q][:, :, lo:hi], a_t[q][:, :, lo:hi], SILU, scale=-1.0)
+
+        def minus_d_silu(q, lo, hi):
+            nc.vector.scalar_tensor_tensor(
+                s_t[q][:, :, lo:hi], sil_t[q][:, :, lo:hi], 1.0, sig_t[q][:, :, lo:hi], SUB, MULT
+            )
+
+        def expert(e):
+            q, x = divmod(e, 2)
+            dab = ring3.tile([P, C, 4], BF16, align_bytes=64, name="dab")
+            for h in range(C // HALF):
+                c0 = x * C + h * HALF
+                dh = psum_h.tile([P, 4, HALF], F32, name="dh")
+                for t in range(4):
+                    nc.tensor.matmul_mx(
+                        out=dh[:, t, :],
+                        lhsT=w2_codes[e][:, t * P : (t + 1) * P].bitcast(FP8X4),
+                        lhsT_scale=w2_scales[e][:, t * P : (t + 1) * P],
+                        rhs=g_codes[q][:, c0 : c0 + HALF].bitcast(FP8X4),
+                        rhs_scale=g_scales[q][:, c0 : c0 + HALF],
+                        start=True,
+                        stop=True,
+                    )
+                nc.vector.scalar_tensor_tensor(
+                    dab[:, h * HALF : (h + 1) * HALF, :],
+                    s_t[q][:, :, c0 : c0 + HALF].rearrange("p t n -> p n t"),
+                    -1.0,
+                    dh[:].rearrange("p t n -> p n t"),
+                    MULT,
+                    MULT,
+                )
+            da_codes = ring3.tile([P, C], U32, align_bytes=64, name="da_codes")
+            da_scales = ring3.tile([P, C], U8, align_bytes=64, name="da_scales")
+            nc.vector.quantize_mx(
+                out=da_codes[:].bitcast(FP8X4), scales=da_scales[:], in_=dab[:].rearrange("p n t -> p (n t)")
+            )
+            dx = psum_x.tile([P, C], F32, name="dx")
+            nc.tensor.matmul_mx(
+                out=dx[:],
+                lhsT=w1_codes[q][:, x * K : (x + 1) * K].bitcast(FP8X4),
+                lhsT_scale=w1_scales[q][:, x * K : (x + 1) * K],
+                rhs=da_codes[:].bitcast(FP8X4),
+                rhs_scale=da_scales[:],
+                start=True,
+                stop=True,
+            )
+            nc.scalar.copy(dx_all[:, e * C : (e + 1) * C], dx[:])
+
+        g4 = gather(0)
+        sigmoid(0, 0, C)
+        sigmoid(0, C, C2)
+        silu_neg(0, 0, C)
+        silu_neg(0, C, C2)
+        gb = cast_g(g4)
+        w2b = cast_w2(0)
+        quant_g(0, gb)
+        quant_w1(0, cast_w1(0))
+        minus_d_silu(0, 0, C)
+        quant_w2(0, w2b)
+        minus_d_silu(0, C, C2)
+        g4 = gather(1)
+        w2b = cast_w2(1)
+        expert(0)
+        quant_w2(1, w2b)
+        silu_neg(1, 0, C2)
+        silu_neg(2, 0, C2)
+        sigmoid(1, 0, C2)
+        sigmoid(2, 0, C2)
+        gb = cast_g(g4)
+        expert(1)
+        w2b = cast_w2(2)
+        quant_g(1, gb)
+        quant_w1(1, cast_w1(1))
+        minus_d_silu(1, 0, C2)
+        quant_w2(2, w2b)
+        g4 = gather(2)
+        w2b = cast_w2(3)
+        expert(2)
+        quant_w2(3, w2b)
+        gb = cast_g(g4)
+        expert(3)
+        w2b = cast_w2(4)
+        quant_g(2, gb)
+        quant_w1(2, cast_w1(2))
+        minus_d_silu(2, 0, C2)
+        quant_w2(4, w2b)
+        w2b = cast_w2(5)
+        expert(4)
+        quant_w2(5, w2b)
+        expert(5)
+
+        tokens = T // 2
+        for u in range(2):
+            first = ring2.tile([P, tokens], F32, name="first")
+            second = ring2.tile([P, tokens], F32, name="second")
+            total = ring2.tile([P, tokens], F32, name="total")
+            cols = slice(u * (tokens // 16), (u + 1) * (tokens // 16))
+            nc.vector.tensor_copy(first[:], dx_all[:].indirect(pos1_t[:, cols]))
+            nc.vector.tensor_copy(second[:], dx_all[:].indirect(pos2_t[:, cols]))
+            adder = nc.gpsimd if u == 0 else nc.vector
+            adder.tensor_tensor(total[:], first[:], second[:], ADD)
+            nc.sync.dma_start(out[:, u * tokens : (u + 1) * tokens], total[:])

@@ -24,7 +24,11 @@ HALF = 128
 FLOPS = 2 * SLOTS * H * (N + K)
 BYTES = 4 * (N * T + H * SLOTS + E * N * H + E * H * K + SLOTS + K * T) + 2 * P * (2 * SLOTS + 0) // 16
 
-W2_ON_VECTOR = (4,)
+W2_ON_VECTOR = (0, 1)
+W2_SPLIT = ()
+W1_ON_SCALAR = (0, 1, 2)
+SILU_FIRST = (2, 3)
+TAIL_CUT = 448
 
 
 def tile_moe_bdx_mlp_silu_kernel(tc, dyT, a, w2, w1, gate, offs, pos1, pos2, out):
@@ -32,8 +36,7 @@ def tile_moe_bdx_mlp_silu_kernel(tc, dyT, a, w2, w1, gate, offs, pos1, pos2, out
     with ExitStack() as ctx:
         lists = ctx.enter_context(tc.tile_pool(name="lists", bufs=1))
         held = ctx.enter_context(tc.tile_pool(name="held", bufs=1))
-        ring2 = ctx.enter_context(tc.tile_pool(name="ring2", bufs=2))
-        ring3 = ctx.enter_context(tc.tile_pool(name="ring3", bufs=3))
+        ring = ctx.enter_context(tc.tile_pool(name="ring", bufs=3))
         psum_h = ctx.enter_context(tc.psum_pool(name="psum_h", bufs=5))
         psum_x = ctx.enter_context(tc.psum_pool(name="psum_x", bufs=3))
 
@@ -44,6 +47,7 @@ def tile_moe_bdx_mlp_silu_kernel(tc, dyT, a, w2, w1, gate, offs, pos1, pos2, out
         gate_t = [held.tile([P, C2], F32, name=f"gate{q}") for q in range(PAIRS)]
         a_t = [held.tile([P, 4, C2], F32, name=f"a{q}") for q in range(PAIRS)]
         s_t = [held.tile([P, 4, C2], F32, name=f"s{q}") for q in range(PAIRS)]
+        g_t = [held.tile([P, 4, C2], F32, name=f"g{q}") for q in range(PAIRS)]
         w2_raw = [held.tile([P, 4, H], F32, name=f"w2_raw{e}") for e in range(E)]
         w1_raw = [held.tile([P, 2, 4, K], F32, name=f"w1_raw{q}") for q in range(PAIRS)]
         g_codes = [held.tile([P, C2], U32, align_bytes=64, name=f"g_codes{q}") for q in range(PAIRS)]
@@ -52,9 +56,10 @@ def tile_moe_bdx_mlp_silu_kernel(tc, dyT, a, w2, w1, gate, offs, pos1, pos2, out
         w2_scales = [held.tile([P, H], U8, align_bytes=64, name=f"w2_scales{e}") for e in range(E)]
         w1_codes = [held.tile([P, 2 * K], U32, align_bytes=64, name=f"w1_codes{q}") for q in range(PAIRS)]
         w1_scales = [held.tile([P, 2 * K], U8, align_bytes=64, name=f"w1_scales{q}") for q in range(PAIRS)]
-        sig_t = [s_t[0], a_t[1], a_t[2]]
-        sil_t = [a_t[0], s_t[1], s_t[2]]
+        da_codes = [held.tile([P, C], U32, align_bytes=64, name=f"da_codes{e}") for e in range(E)]
+        da_scales = [held.tile([P, C], U8, align_bytes=64, name=f"da_scales{e}") for e in range(E)]
         dx_all = held.tile([P, SLOTS], F32, name="dx_all")
+        live = {}
         warm = held.tile([P, 1], F32, name="warm")
 
         nc.vector.memset(warm[:], 0.0)
@@ -78,184 +83,243 @@ def tile_moe_bdx_mlp_silu_kernel(tc, dyT, a, w2, w1, gate, offs, pos1, pos2, out
         def load_w1(q):
             nc.sync.dma_start(w1_raw[q][:], w1[2 * q : 2 * q + 2].rearrange("e (p j) k -> p e j k", j=4))
 
-        nc.sync.dma_start(offs_t[:], offs)
-        load_dy(0)
-        load_gate(0)
-        load_a(0, 0, C)
-        load_dy(1)
-        load_dy(2)
-        load_dy(3)
-        load_a(0, C, C2)
-        load_w2(0)
-        load_w1(0)
-        load_gate(1)
-        load_w2(1)
-        load_a(1, 0, C2)
-        load_a(2, 0, C2)
-        load_gate(2)
-        load_w2(2)
-        load_w1(1)
-        load_w2(3)
-        load_w2(4)
-        load_w1(2)
-        load_w2(5)
-        nc.sync.dma_start(pos1_t[:], pos1)
-        nc.sync.dma_start(pos2_t[:], pos2)
-
-        def gather(q):
-            g4 = ring2.tile([P, 4, C2], F32, name="g4")
-            for t in range(4):
-                nc.vector.tensor_tensor(
-                    g4[:, t, :],
-                    dy_t[t][:].indirect(offs_t[:, q * (C2 // 16) : (q + 1) * (C2 // 16)]),
-                    gate_t[q][:],
-                    MULT,
-                )
-            return g4
-
-        def cast_g(g4):
-            gb = ring2.tile([P, C2, 4], BF16, align_bytes=64, name="gb")
-            nc.scalar.copy(
-                gb[:].rearrange("p (c i) t -> p c t i", i=4), g4[:].rearrange("p t (c i) -> p c t i", i=4)
+        def gather(q, t):
+            nc.vector.tensor_tensor(
+                g_t[q][:, t, :],
+                dy_t[t][:].indirect(offs_t[:, q * (C2 // 16) : (q + 1) * (C2 // 16)]),
+                gate_t[q][:],
+                MULT,
             )
-            return gb
 
-        def quant_g(q, gb):
+        def cast_g(q):
+            gb = ring.tile([P, C2, 4], BF16, align_bytes=64, name="gb")
+            live["gb", q] = gb
+            nc.scalar.copy(
+                gb[:].rearrange("p (c i) t -> p c t i", i=4), g_t[q][:].rearrange("p t (c i) -> p c t i", i=4)
+            )
+
+        def quant_g(q):
             nc.vector.quantize_mx(
-                out=g_codes[q][:].bitcast(FP8X4), scales=g_scales[q][:], in_=gb[:].rearrange("p n j -> p (n j)")
+                out=g_codes[q][:].bitcast(FP8X4),
+                scales=g_scales[q][:],
+                in_=live["gb", q][:].rearrange("p n j -> p (n j)"),
             )
 
         def cast_w2(e):
-            w2b = ring3.tile([P, H, 4], BF16, align_bytes=64, name="w2b")
+            w2b = ring.tile([P, H, 4], BF16, align_bytes=64, name="w2b")
+            live["w2b", e] = w2b
             dst = w2b[:].rearrange("p (t m) j -> p m j t", t=4)
             src = w2_raw[e][:].rearrange("p j (m t) -> p m j t", t=4)
             if e in W2_ON_VECTOR:
                 nc.vector.tensor_copy(dst, src)
+            elif e in W2_SPLIT:
+                nc.scalar.copy(dst[:, 0 : P // 2], src[:, 0 : P // 2])
+                nc.vector.tensor_copy(dst[:, P // 2 : P], src[:, P // 2 : P])
             else:
                 nc.scalar.copy(dst, src)
-            return w2b
 
-        def quant_w2(e, w2b):
+        def quant_w2(e):
             nc.vector.quantize_mx(
-                out=w2_codes[e][:].bitcast(FP8X4), scales=w2_scales[e][:], in_=w2b[:].rearrange("p i j -> p (i j)")
+                out=w2_codes[e][:].bitcast(FP8X4),
+                scales=w2_scales[e][:],
+                in_=live["w2b", e][:].rearrange("p i j -> p (i j)"),
             )
 
         def cast_w1(q):
-            w1b = ring2.tile([P, 2, K, 4], BF16, align_bytes=64, name="w1b")
-            nc.vector.tensor_copy(
-                w1b[:].rearrange("p e (c i) j -> p e c j i", i=4),
-                w1_raw[q][:].rearrange("p e j (c i) -> p e c j i", i=4),
-            )
-            return w1b
+            w1b = ring.tile([P, 2, K, 4], BF16, align_bytes=64, bufs=2, name="w1b")
+            live["w1b", q] = w1b
+            if q in W1_ON_SCALAR:
+                nc.scalar.copy(
+                    w1b[:], w1_raw[q][:].rearrange("p e j k -> p e k j")
+                )
+            else:
+                nc.vector.tensor_copy(
+                    w1b[:].rearrange("p e (c i) j -> p e c j i", i=4),
+                    w1_raw[q][:].rearrange("p e j (c i) -> p e c j i", i=4),
+                )
 
-        def quant_w1(q, w1b):
+        def quant_w1(q):
             nc.vector.quantize_mx(
-                out=w1_codes[q][:].bitcast(FP8X4), scales=w1_scales[q][:], in_=w1b[:].rearrange("p e k j -> p (e k j)")
+                out=w1_codes[q][:].bitcast(FP8X4),
+                scales=w1_scales[q][:],
+                in_=live["w1b", q][:].rearrange("p e k j -> p (e k j)"),
             )
 
-        def sigmoid(q, lo, hi):
-            nc.scalar.activation(sig_t[q][:, :, lo:hi], a_t[q][:, :, lo:hi], SIGMOID)
+        def functions_of(e):
+            q, x = divmod(e, 2)
+            cols = slice(x * C, (x + 1) * C)
+            saved, fresh = a_t[q][:, :, cols], s_t[q][:, :, cols]
+            return (saved, saved, fresh) if e in SILU_FIRST else (saved, fresh, saved)
 
-        def silu_neg(q, lo, hi):
-            nc.scalar.activation(sil_t[q][:, :, lo:hi], a_t[q][:, :, lo:hi], SILU, scale=-1.0)
+        def sigmoid(e):
+            saved, sig, sil = functions_of(e)
+            nc.scalar.activation(sig, saved, SIGMOID)
+
+        def silu_neg(e):
+            saved, sig, sil = functions_of(e)
+            nc.scalar.activation(sil, saved, SILU, scale=-1.0)
 
         def minus_d_silu(q, lo, hi):
+            one, two = a_t[q][:, :, lo:hi], s_t[q][:, :, lo:hi]
+            sil, sig = (two, one) if 2 * q + lo // C in SILU_FIRST else (one, two)
+            nc.vector.scalar_tensor_tensor(two, sil, 1.0, sig, SUB, MULT)
+
+        def minus_d_silu_from_sigmoid(q, lo, hi):
+            saved, sig = a_t[q][:, :, lo:hi], s_t[q][:, :, lo:hi]
+            nc.vector.scalar_tensor_tensor(saved, sig, 1.0, saved, SUB, MULT)
+            nc.vector.scalar_tensor_tensor(sig, saved, 1.0, sig, SUB, MULT)
+
+        def first_product(e, h):
+            q, x = divmod(e, 2)
+            c0 = x * C + h * HALF
+            if ("dab", e) not in live:
+                dab = ring.tile([P, C, 4], BF16, align_bytes=64, bufs=4, name="dab")
+                live["dab", e] = dab
+            dh = psum_h.tile([P, 4, HALF], F32, name="dh")
+            for t in range(4):
+                nc.tensor.matmul_mx(
+                    out=dh[:, t, :],
+                    lhsT=w2_codes[e][:, t * P : (t + 1) * P].bitcast(FP8X4),
+                    lhsT_scale=w2_scales[e][:, t * P : (t + 1) * P],
+                    rhs=g_codes[q][:, c0 : c0 + HALF].bitcast(FP8X4),
+                    rhs_scale=g_scales[q][:, c0 : c0 + HALF],
+                    start=True,
+                    stop=True,
+                )
             nc.vector.scalar_tensor_tensor(
-                s_t[q][:, :, lo:hi], sil_t[q][:, :, lo:hi], 1.0, sig_t[q][:, :, lo:hi], SUB, MULT
+                live["dab", e][:, h * HALF : (h + 1) * HALF, :],
+                s_t[q][:, :, c0 : c0 + HALF].rearrange("p t n -> p n t"),
+                -1.0,
+                dh[:].rearrange("p t n -> p n t"),
+                MULT,
+                MULT,
             )
 
-        def expert(e):
-            q, x = divmod(e, 2)
-            dab = ring3.tile([P, C, 4], BF16, align_bytes=64, name="dab")
-            for h in range(C // HALF):
-                c0 = x * C + h * HALF
-                dh = psum_h.tile([P, 4, HALF], F32, name="dh")
-                for t in range(4):
-                    nc.tensor.matmul_mx(
-                        out=dh[:, t, :],
-                        lhsT=w2_codes[e][:, t * P : (t + 1) * P].bitcast(FP8X4),
-                        lhsT_scale=w2_scales[e][:, t * P : (t + 1) * P],
-                        rhs=g_codes[q][:, c0 : c0 + HALF].bitcast(FP8X4),
-                        rhs_scale=g_scales[q][:, c0 : c0 + HALF],
-                        start=True,
-                        stop=True,
-                    )
-                nc.vector.scalar_tensor_tensor(
-                    dab[:, h * HALF : (h + 1) * HALF, :],
-                    s_t[q][:, :, c0 : c0 + HALF].rearrange("p t n -> p n t"),
-                    -1.0,
-                    dh[:].rearrange("p t n -> p n t"),
-                    MULT,
-                    MULT,
-                )
-            da_codes = ring3.tile([P, C], U32, align_bytes=64, name="da_codes")
-            da_scales = ring3.tile([P, C], U8, align_bytes=64, name="da_scales")
+        def quant_da(e):
             nc.vector.quantize_mx(
-                out=da_codes[:].bitcast(FP8X4), scales=da_scales[:], in_=dab[:].rearrange("p n t -> p (n t)")
+                out=da_codes[e][:].bitcast(FP8X4),
+                scales=da_scales[e][:],
+                in_=live["dab", e][:].rearrange("p n t -> p (n t)"),
             )
+
+        def second_product(e):
+            q, x = divmod(e, 2)
             dx = psum_x.tile([P, C], F32, name="dx")
             nc.tensor.matmul_mx(
                 out=dx[:],
                 lhsT=w1_codes[q][:, x * K : (x + 1) * K].bitcast(FP8X4),
                 lhsT_scale=w1_scales[q][:, x * K : (x + 1) * K],
-                rhs=da_codes[:].bitcast(FP8X4),
-                rhs_scale=da_scales[:],
+                rhs=da_codes[e][:].bitcast(FP8X4),
+                rhs_scale=da_scales[e][:],
                 start=True,
                 stop=True,
             )
             nc.scalar.copy(dx_all[:, e * C : (e + 1) * C], dx[:])
 
-        g4 = gather(0)
-        sigmoid(0, 0, C)
-        sigmoid(0, C, C2)
-        silu_neg(0, 0, C)
-        silu_neg(0, C, C2)
-        gb = cast_g(g4)
-        w2b = cast_w2(0)
-        quant_g(0, gb)
-        quant_w1(0, cast_w1(0))
-        minus_d_silu(0, 0, C)
-        quant_w2(0, w2b)
-        minus_d_silu(0, C, C2)
-        g4 = gather(1)
-        w2b = cast_w2(1)
-        expert(0)
-        quant_w2(1, w2b)
-        silu_neg(1, 0, C2)
-        silu_neg(2, 0, C2)
-        sigmoid(1, 0, C2)
-        sigmoid(2, 0, C2)
-        gb = cast_g(g4)
-        expert(1)
-        w2b = cast_w2(2)
-        quant_g(1, gb)
-        quant_w1(1, cast_w1(1))
+        load_a(0, 0, C)
+        load_a(0, C, C2)
+        load_a(1, 0, C2)
+        load_dy(3)
+        load_gate(2)
+        nc.sync.dma_start(offs_t[:], offs)
+        load_gate(0)
+        load_gate(1)
+        load_dy(1)
+        load_w2(3)
+        load_dy(0)
+        nc.sync.dma_start(pos1_t[:], pos1)
+        load_dy(2)
+        nc.sync.dma_start(pos2_t[:], pos2)
+        load_w1(0)
+        load_w2(0)
+        load_w2(2)
+        load_w2(1)
+        load_w2(4)
+        load_a(2, 0, C2)
+        load_w2(5)
+        load_w1(2)
+        load_w1(1)
+        silu_neg(3)
+        sigmoid(0)
+        gather(2, 0)
+        gather(0, 0)
+        cast_w2(3)
+        sigmoid(5)
+        gather(1, 1)
+        gather(2, 1)
+        gather(1, 2)
+        sigmoid(1)
+        silu_neg(2)
+        cast_w1(0)
+        gather(0, 3)
+        silu_neg(1)
+        gather(0, 1)
+        gather(2, 3)
+        gather(1, 0)
+        gather(2, 2)
+        sigmoid(4)
+        sigmoid(3)
+        quant_w2(3)
+        gather(0, 2)
+        gather(1, 3)
+        cast_g(1)
+        cast_w2(0)
+        quant_w2(0)
+        sigmoid(2)
         minus_d_silu(1, 0, C2)
-        quant_w2(2, w2b)
-        g4 = gather(2)
-        w2b = cast_w2(3)
-        expert(2)
-        quant_w2(3, w2b)
-        gb = cast_g(g4)
-        expert(3)
-        w2b = cast_w2(4)
-        quant_g(2, gb)
-        quant_w1(2, cast_w1(2))
+        cast_w2(1)
+        minus_d_silu_from_sigmoid(0, 0, C)
+        quant_w2(1)
+        quant_g(1)
+        first_product(3, 1)
+        cast_g(0)
+        quant_g(0)
+        minus_d_silu(0, C, C2)
+        first_product(0, 1)
+        cast_w2(2)
+        quant_w2(2)
+        first_product(0, 0)
+        quant_w1(0)
+        first_product(1, 1)
+        silu_neg(5)
+        first_product(3, 0)
+        quant_da(3)
+        cast_g(2)
+        first_product(1, 0)
+        quant_da(1)
+        second_product(1)
+        quant_g(2)
+        cast_w2(4)
+        first_product(2, 1)
+        quant_da(0)
+        quant_w2(4)
+        first_product(2, 0)
+        silu_neg(4)
         minus_d_silu(2, 0, C2)
-        quant_w2(4, w2b)
-        w2b = cast_w2(5)
-        expert(4)
-        quant_w2(5, w2b)
-        expert(5)
+        second_product(0)
+        first_product(4, 1)
+        first_product(4, 0)
+        cast_w2(5)
+        quant_w2(5)
+        first_product(5, 0)
+        cast_w1(1)
+        quant_da(2)
+        quant_w1(1)
+        second_product(3)
+        first_product(5, 1)
+        quant_da(5)
+        second_product(2)
+        cast_w1(2)
+        quant_w1(2)
+        second_product(5)
+        quant_da(4)
+        second_product(4)
 
-        tokens = T // 2
-        for u in range(2):
-            first = ring2.tile([P, tokens], F32, name="first")
-            second = ring2.tile([P, tokens], F32, name="second")
-            total = ring2.tile([P, tokens], F32, name="total")
-            cols = slice(u * (tokens // 16), (u + 1) * (tokens // 16))
-            nc.vector.tensor_copy(first[:], dx_all[:].indirect(pos1_t[:, cols]))
-            nc.vector.tensor_copy(second[:], dx_all[:].indirect(pos2_t[:, cols]))
-            adder = nc.gpsimd if u == 0 else nc.vector
-            adder.tensor_tensor(total[:], first[:], second[:], ADD)
-            nc.sync.dma_start(out[:, u * tokens : (u + 1) * tokens], total[:])
+        first = held.tile([P, T], F32, name="first")
+        second = held.tile([P, T], F32, name="second")
+        total = held.tile([P, T], F32, name="total")
+        nc.vector.tensor_copy(first[:], dx_all[:].indirect(pos1_t[:]))
+        for lo, hi, adder in ((0, TAIL_CUT, nc.gpsimd), (TAIL_CUT, T, nc.vector)):
+            nc.vector.tensor_copy(second[:, lo:hi], dx_all[:].indirect(pos2_t[:, lo // 16 : hi // 16]))
+            adder.tensor_tensor(total[:, lo:hi], first[:, lo:hi], second[:, lo:hi], ADD)
+            nc.sync.dma_start(out[:, lo:hi], total[:, lo:hi])

@@ -24,10 +24,10 @@ HALF = 128
 FLOPS = 2 * SLOTS * H * (N + K)
 BYTES = 4 * (N * T + H * SLOTS + E * N * H + E * H * K + SLOTS + K * T) + 2 * P * (2 * SLOTS + 0) // 16
 
-W2_ON_VECTOR = (0, 1)
-W2_SPLIT = ()
+W2_ON_VECTOR = (3,)
+W2_SPLIT = (2, 5)
 W1_ON_SCALAR = (0, 1, 2)
-SILU_FIRST = (2, 3)
+SILU_FIRST = (4,)
 TAIL_CUT = 448
 
 
@@ -216,104 +216,105 @@ def tile_moe_bdx_mlp_silu_kernel(tc, dyT, a, w2, w1, gate, offs, pos1, pos2, out
             )
             nc.scalar.copy(dx_all[:, e * C : (e + 1) * C], dx[:])
 
-        load_a(0, 0, C)
-        load_a(0, C, C2)
-        load_a(1, 0, C2)
-        load_dy(3)
-        load_gate(2)
+        load_dy(1)
         nc.sync.dma_start(offs_t[:], offs)
         load_gate(0)
         load_gate(1)
-        load_dy(1)
-        load_w2(3)
-        load_dy(0)
-        nc.sync.dma_start(pos1_t[:], pos1)
-        load_dy(2)
-        nc.sync.dma_start(pos2_t[:], pos2)
-        load_w1(0)
-        load_w2(0)
-        load_w2(2)
-        load_w2(1)
-        load_w2(4)
+        load_a(0, C, C2)
+        load_gate(2)
+        load_dy(3)
         load_a(2, 0, C2)
+        load_dy(2)
+        load_a(1, 0, C2)
+        load_a(0, 0, C)
+        load_dy(0)
+        load_w2(2)
+        load_w2(3)
+        nc.sync.dma_start(pos1_t[:], pos1)
+        nc.sync.dma_start(pos2_t[:], pos2)
         load_w2(5)
-        load_w1(2)
+        load_w2(4)
+        load_w2(1)
+        load_w2(0)
         load_w1(1)
-        silu_neg(3)
-        sigmoid(0)
-        gather(2, 0)
-        gather(0, 0)
+        load_w1(0)
+        load_w1(2)
+        gather(1, 3)
+        silu_neg(4)
+        sigmoid(2)
+        sigmoid(3)
         cast_w2(3)
         sigmoid(5)
-        gather(1, 1)
-        gather(2, 1)
-        gather(1, 2)
-        sigmoid(1)
-        silu_neg(2)
-        cast_w1(0)
-        gather(0, 3)
-        silu_neg(1)
-        gather(0, 1)
-        gather(2, 3)
-        gather(1, 0)
-        gather(2, 2)
         sigmoid(4)
-        sigmoid(3)
+        cast_w2(2)
+        sigmoid(0)
         quant_w2(3)
-        gather(0, 2)
-        gather(1, 3)
-        cast_g(1)
-        cast_w2(0)
-        quant_w2(0)
-        sigmoid(2)
+        silu_neg(3)
+        silu_neg(0)
+        gather(1, 2)
+        gather(2, 0)
+        quant_w2(2)
+        silu_neg(5)
+        minus_d_silu(2, 0, C)
+        gather(2, 2)
+        silu_neg(2)
+        sigmoid(1)
+        silu_neg(1)
+        gather(0, 3)
+        minus_d_silu(0, 0, C2)
+        gather(1, 0)
+        gather(2, 3)
+        cast_w2(5)
+        gather(1, 1)
+        gather(0, 1)
         minus_d_silu(1, 0, C2)
-        cast_w2(1)
-        minus_d_silu_from_sigmoid(0, 0, C)
-        quant_w2(1)
+        quant_w2(5)
+        gather(0, 2)
+        gather(2, 1)
+        cast_g(2)
+        quant_g(2)
+        minus_d_silu(2, C, C2)
+        cast_g(1)
         quant_g(1)
+        first_product(5, 1)
+        first_product(5, 0)
+        first_product(2, 1)
+        first_product(2, 0)
+        quant_da(2)
+        cast_w2(4)
+        quant_w2(4)
+        gather(0, 0)
         first_product(3, 1)
+        cast_w2(1)
+        quant_w2(1)
+        first_product(4, 1)
+        quant_da(5)
+        first_product(4, 0)
         cast_g(0)
         quant_g(0)
-        minus_d_silu(0, C, C2)
-        first_product(0, 1)
-        cast_w2(2)
-        quant_w2(2)
-        first_product(0, 0)
-        quant_w1(0)
-        first_product(1, 1)
-        silu_neg(5)
         first_product(3, 0)
         quant_da(3)
-        cast_g(2)
+        quant_da(4)
+        first_product(1, 1)
+        cast_w2(0)
+        quant_w2(0)
         first_product(1, 0)
-        quant_da(1)
-        second_product(1)
-        quant_g(2)
-        cast_w2(4)
-        first_product(2, 1)
-        quant_da(0)
-        quant_w2(4)
-        first_product(2, 0)
-        silu_neg(4)
-        minus_d_silu(2, 0, C2)
-        second_product(0)
-        first_product(4, 1)
-        first_product(4, 0)
-        cast_w2(5)
-        quant_w2(5)
-        first_product(5, 0)
-        cast_w1(1)
-        quant_da(2)
-        quant_w1(1)
-        second_product(3)
-        first_product(5, 1)
-        quant_da(5)
-        second_product(2)
         cast_w1(2)
         quant_w1(2)
+        quant_da(1)
         second_product(5)
-        quant_da(4)
+        cast_w1(1)
+        first_product(0, 0)
+        quant_w1(1)
+        first_product(0, 1)
+        second_product(2)
+        cast_w1(0)
         second_product(4)
+        quant_w1(0)
+        second_product(1)
+        quant_da(0)
+        second_product(0)
+        second_product(3)
 
         first = held.tile([P, T], F32, name="first")
         second = held.tile([P, T], F32, name="second")

from contextlib import ExitStack

import concourse.mybir as mybir

F32 = mybir.dt.float32
BF16 = mybir.dt.bfloat16
U32 = mybir.dt.uint32
U16 = mybir.dt.uint16
U8 = mybir.dt.uint8
FP8X4 = mybir.dt.float8_e4m3fn_x4
ADD = mybir.AluOpType.add
SUB = mybir.AluOpType.subtract
MULT = mybir.AluOpType.mult
SIGMOID = mybir.ActivationFunctionType.Sigmoid
SILU = mybir.ActivationFunctionType.Silu

P = 128
K, T, E, C, H, N = 128, 768, 6, 256, 512, 512
SLOTS = E * C
PAIRS = E // 2
C2 = 2 * C
HALF = 128

FLOPS = 2 * SLOTS * H * (N + K)
BYTES = 4 * (N * T + H * SLOTS + E * N * H + E * H * K + SLOTS + K * T) + 2 * P * (2 * SLOTS + 0) // 16

W2_ON_VECTOR = (3,)
W2_SPLIT = (2, 5)
W1_ON_SCALAR = (0, 1, 2)
SILU_FIRST = (4,)
TAIL_CUT = 448


def tile_moe_bdx_mlp_silu_kernel(tc, dyT, a, w2, w1, gate, offs, pos1, pos2, out):
    nc = tc.nc
    with ExitStack() as ctx:
        lists = ctx.enter_context(tc.tile_pool(name="lists", bufs=1))
        held = ctx.enter_context(tc.tile_pool(name="held", bufs=1))
        ring = ctx.enter_context(tc.tile_pool(name="ring", bufs=3))
        psum_h = ctx.enter_context(tc.psum_pool(name="psum_h", bufs=5))
        psum_x = ctx.enter_context(tc.psum_pool(name="psum_x", bufs=3))

        offs_t = lists.tile([P, SLOTS // 16], U16, name="offs_t")
        pos1_t = lists.tile([P, T // 16], U16, name="pos1_t")
        pos2_t = lists.tile([P, T // 16], U16, name="pos2_t")
        dy_t = [held.tile([P, T], F32, name=f"dy{t}") for t in range(4)]
        gate_t = [held.tile([P, C2], F32, name=f"gate{q}") for q in range(PAIRS)]
        a_t = [held.tile([P, 4, C2], F32, name=f"a{q}") for q in range(PAIRS)]
        s_t = [held.tile([P, 4, C2], F32, name=f"s{q}") for q in range(PAIRS)]
        g_t = [held.tile([P, 4, C2], F32, name=f"g{q}") for q in range(PAIRS)]
        w2_raw = [held.tile([P, 4, H], F32, name=f"w2_raw{e}") for e in range(E)]
        w1_raw = [held.tile([P, 2, 4, K], F32, name=f"w1_raw{q}") for q in range(PAIRS)]
        g_codes = [held.tile([P, C2], U32, align_bytes=64, name=f"g_codes{q}") for q in range(PAIRS)]
        g_scales = [held.tile([P, C2], U8, align_bytes=64, name=f"g_scales{q}") for q in range(PAIRS)]
        w2_codes = [held.tile([P, H], U32, align_bytes=64, name=f"w2_codes{e}") for e in range(E)]
        w2_scales = [held.tile([P, H], U8, align_bytes=64, name=f"w2_scales{e}") for e in range(E)]
        w1_codes = [held.tile([P, 2 * K], U32, align_bytes=64, name=f"w1_codes{q}") for q in range(PAIRS)]
        w1_scales = [held.tile([P, 2 * K], U8, align_bytes=64, name=f"w1_scales{q}") for q in range(PAIRS)]
        da_codes = [held.tile([P, C], U32, align_bytes=64, name=f"da_codes{e}") for e in range(E)]
        da_scales = [held.tile([P, C], U8, align_bytes=64, name=f"da_scales{e}") for e in range(E)]
        dx_all = held.tile([P, SLOTS], F32, name="dx_all")
        live = {}
        warm = held.tile([P, 1], F32, name="warm")

        nc.vector.memset(warm[:], 0.0)
        nc.scalar.activation(warm[:], warm[:], SIGMOID)

        dy_rows = dyT.rearrange("(p t) c -> t p c", t=4)
        a_rows = a.rearrange("(p t) s -> p t s", t=4)

        def load_dy(t):
            nc.sync.dma_start(dy_t[t][:], dy_rows[t])

        def load_gate(q):
            nc.sync.dma_start(gate_t[q][:], gate[0:P, q * C2 : (q + 1) * C2])

        def load_a(q, lo, hi):
            nc.sync.dma_start(a_t[q][:, :, lo:hi], a_rows[:, :, q * C2 + lo : q * C2 + hi])

        def load_w2(e):
            nc.sync.dma_start(w2_raw[e][:], w2[e].rearrange("(p j) i -> p j i", j=4))

        def load_w1(q):
            nc.sync.dma_start(w1_raw[q][:], w1[2 * q : 2 * q + 2].rearrange("e (p j) k -> p e j k", j=4))

        def gather(q, t):
            nc.vector.tensor_tensor(
                g_t[q][:, t, :],
                dy_t[t][:].indirect(offs_t[:, q * (C2 // 16) : (q + 1) * (C2 // 16)]),
                gate_t[q][:],
                MULT,
            )

        def cast_g(q):
            gb = ring.tile([P, C2, 4], BF16, align_bytes=64, name="gb")
            live["gb", q] = gb
            nc.scalar.copy(
                gb[:].rearrange("p (c i) t -> p c t i", i=4), g_t[q][:].rearrange("p t (c i) -> p c t i", i=4)
            )

        def quant_g(q):
            nc.vector.quantize_mx(
                out=g_codes[q][:].bitcast(FP8X4),
                scales=g_scales[q][:],
                in_=live["gb", q][:].rearrange("p n j -> p (n j)"),
            )

        def cast_w2(e):
            w2b = ring.tile([P, H, 4], BF16, align_bytes=64, name="w2b")
            live["w2b", e] = w2b
            dst = w2b[:].rearrange("p (t m) j -> p m j t", t=4)
            src = w2_raw[e][:].rearrange("p j (m t) -> p m j t", t=4)
            if e in W2_ON_VECTOR:
                nc.vector.tensor_copy(dst, src)
            elif e in W2_SPLIT:
                nc.scalar.copy(dst[:, 0 : P // 2], src[:, 0 : P // 2])
                nc.vector.tensor_copy(dst[:, P // 2 : P], src[:, P // 2 : P])
            else:
                nc.scalar.copy(dst, src)

        def quant_w2(e):
            nc.vector.quantize_mx(
                out=w2_codes[e][:].bitcast(FP8X4),
                scales=w2_scales[e][:],
                in_=live["w2b", e][:].rearrange("p i j -> p (i j)"),
            )

        def cast_w1(q):
            w1b = ring.tile([P, 2, K, 4], BF16, align_bytes=64, bufs=2, name="w1b")
            live["w1b", q] = w1b
            if q in W1_ON_SCALAR:
                nc.scalar.copy(
                    w1b[:], w1_raw[q][:].rearrange("p e j k -> p e k j")
                )
            else:
                nc.vector.tensor_copy(
                    w1b[:].rearrange("p e (c i) j -> p e c j i", i=4),
                    w1_raw[q][:].rearrange("p e j (c i) -> p e c j i", i=4),
                )

        def quant_w1(q):
            nc.vector.quantize_mx(
                out=w1_codes[q][:].bitcast(FP8X4),
                scales=w1_scales[q][:],
                in_=live["w1b", q][:].rearrange("p e k j -> p (e k j)"),
            )

        def functions_of(e):
            q, x = divmod(e, 2)
            cols = slice(x * C, (x + 1) * C)
            saved, fresh = a_t[q][:, :, cols], s_t[q][:, :, cols]
            return (saved, saved, fresh) if e in SILU_FIRST else (saved, fresh, saved)

        def sigmoid(e):
            saved, sig, sil = functions_of(e)
            nc.scalar.activation(sig, saved, SIGMOID)

        def silu_neg(e):
            saved, sig, sil = functions_of(e)
            nc.scalar.activation(sil, saved, SILU, scale=-1.0)

        def minus_d_silu(q, lo, hi):
            one, two = a_t[q][:, :, lo:hi], s_t[q][:, :, lo:hi]
            sil, sig = (two, one) if 2 * q + lo // C in SILU_FIRST else (one, two)
            nc.vector.scalar_tensor_tensor(two, sil, 1.0, sig, SUB, MULT)

        def minus_d_silu_from_sigmoid(q, lo, hi):
            saved, sig = a_t[q][:, :, lo:hi], s_t[q][:, :, lo:hi]
            nc.vector.scalar_tensor_tensor(saved, sig, 1.0, saved, SUB, MULT)
            nc.vector.scalar_tensor_tensor(sig, saved, 1.0, sig, SUB, MULT)

        def first_product(e, h):
            q, x = divmod(e, 2)
            c0 = x * C + h * HALF
            if ("dab", e) not in live:
                dab = ring.tile([P, C, 4], BF16, align_bytes=64, bufs=4, name="dab")
                live["dab", e] = dab
            dh = psum_h.tile([P, 4, HALF], F32, name="dh")
            for t in range(4):
                nc.tensor.matmul_mx(
                    out=dh[:, t, :],
                    lhsT=w2_codes[e][:, t * P : (t + 1) * P].bitcast(FP8X4),
                    lhsT_scale=w2_scales[e][:, t * P : (t + 1) * P],
                    rhs=g_codes[q][:, c0 : c0 + HALF].bitcast(FP8X4),
                    rhs_scale=g_scales[q][:, c0 : c0 + HALF],
                    start=True,
                    stop=True,
                )
            nc.vector.scalar_tensor_tensor(
                live["dab", e][:, h * HALF : (h + 1) * HALF, :],
                s_t[q][:, :, c0 : c0 + HALF].rearrange("p t n -> p n t"),
                -1.0,
                dh[:].rearrange("p t n -> p n t"),
                MULT,
                MULT,
            )

        def quant_da(e):
            nc.vector.quantize_mx(
                out=da_codes[e][:].bitcast(FP8X4),
                scales=da_scales[e][:],
                in_=live["dab", e][:].rearrange("p n t -> p (n t)"),
            )

        def second_product(e):
            q, x = divmod(e, 2)
            dx = psum_x.tile([P, C], F32, name="dx")
            nc.tensor.matmul_mx(
                out=dx[:],
                lhsT=w1_codes[q][:, x * K : (x + 1) * K].bitcast(FP8X4),
                lhsT_scale=w1_scales[q][:, x * K : (x + 1) * K],
                rhs=da_codes[e][:].bitcast(FP8X4),
                rhs_scale=da_scales[e][:],
                start=True,
                stop=True,
            )
            nc.scalar.copy(dx_all[:, e * C : (e + 1) * C], dx[:])

        load_dy(1)
        nc.sync.dma_start(offs_t[:], offs)
        load_gate(0)
        load_gate(1)
        load_a(0, C, C2)
        load_gate(2)
        load_dy(3)
        load_a(2, 0, C2)
        load_dy(2)
        load_a(1, 0, C2)
        load_a(0, 0, C)
        load_dy(0)
        load_w2(2)
        load_w2(3)
        nc.sync.dma_start(pos1_t[:], pos1)
        nc.sync.dma_start(pos2_t[:], pos2)
        load_w2(5)
        load_w2(4)
        load_w2(1)
        load_w2(0)
        load_w1(1)
        load_w1(0)
        load_w1(2)
        gather(1, 3)
        silu_neg(4)
        sigmoid(2)
        sigmoid(3)
        cast_w2(3)
        sigmoid(5)
        sigmoid(4)
        cast_w2(2)
        sigmoid(0)
        quant_w2(3)
        silu_neg(3)
        silu_neg(0)
        gather(1, 2)
        gather(2, 0)
        quant_w2(2)
        silu_neg(5)
        minus_d_silu(2, 0, C)
        gather(2, 2)
        silu_neg(2)
        sigmoid(1)
        silu_neg(1)
        gather(0, 3)
        minus_d_silu(0, 0, C2)
        gather(1, 0)
        gather(2, 3)
        cast_w2(5)
        gather(1, 1)
        gather(0, 1)
        minus_d_silu(1, 0, C2)
        quant_w2(5)
        gather(0, 2)
        gather(2, 1)
        cast_g(2)
        quant_g(2)
        minus_d_silu(2, C, C2)
        cast_g(1)
        quant_g(1)
        first_product(5, 1)
        first_product(5, 0)
        first_product(2, 1)
        first_product(2, 0)
        quant_da(2)
        cast_w2(4)
        quant_w2(4)
        gather(0, 0)
        first_product(3, 1)
        cast_w2(1)
        quant_w2(1)
        first_product(4, 1)
        quant_da(5)
        first_product(4, 0)
        cast_g(0)
        quant_g(0)
        first_product(3, 0)
        quant_da(3)
        quant_da(4)
        first_product(1, 1)
        cast_w2(0)
        quant_w2(0)
        first_product(1, 0)
        cast_w1(2)
        quant_w1(2)
        quant_da(1)
        second_product(5)
        cast_w1(1)
        first_product(0, 0)
        quant_w1(1)
        first_product(0, 1)
        second_product(2)
        cast_w1(0)
        second_product(4)
        quant_w1(0)
        second_product(1)
        quant_da(0)
        second_product(0)
        second_product(3)

        first = held.tile([P, T], F32, name="first")
        second = held.tile([P, T], F32, name="second")
        total = held.tile([P, T], F32, name="total")
        nc.vector.tensor_copy(first[:], dx_all[:].indirect(pos1_t[:]))
        for lo, hi, adder in ((0, TAIL_CUT, nc.gpsimd), (TAIL_CUT, T, nc.vector)):
            nc.vector.tensor_copy(second[:, lo:hi], dx_all[:].indirect(pos2_t[:, lo // 16 : hi // 16]))
            adder.tensor_tensor(total[:, lo:hi], first[:, lo:hi], second[:, lo:hi], ADD)
            nc.sync.dma_start(out[:, lo:hi], total[:, lo:hi])
